import numpy as np
import ml_dtypes


def mxq(x, axis, fmt="e4m3"):
    dtype, down = {"e4m3": (ml_dtypes.float8_e4m3fn, 7), "e5m2": (ml_dtypes.float8_e5m2, 14)}[fmt]
    v = np.moveaxis(np.asarray(x, np.float32).astype(ml_dtypes.bfloat16).astype(np.float64), axis, -1)
    blocks = v.reshape(v.shape[:-1] + (-1, 32))
    amax = np.abs(blocks).max(-1, keepdims=True)
    byte = np.maximum(np.where(amax > 0, np.frexp(amax)[1] - 1 + 127, 0) - down, 1)
    scale = np.exp2(byte - 127.0)
    codes = (blocks / scale).astype(np.float32).astype(dtype).astype(np.float64)
    return np.moveaxis((codes * scale).reshape(v.shape), -1, axis)


WIDE = False


def mx_kscale(k):
    if not WIDE:
        return np.ones(k)
    levels = np.array([24, -24, 12, -12, 0])
    if k % 512:
        return np.exp2(np.random.permutation(np.resize(levels, k // 32))).repeat(32)
    a = np.empty((k // 512, 16))
    for p in range(k // 512):
        a[p, :8] = np.random.permutation(np.resize(levels, 8))
        for g in range(8):
            far = levels[np.abs(levels - a[p, g]) >= 10]
            a[p, g + 8] = far[np.random.randint(len(far))]
    return np.exp2(a.ravel()).repeat(32)


def f64(x):
    return np.asarray(x).astype(np.float64)


def striped8(idx):
    return np.concatenate([v.reshape(-1, 16).T for v in idx]).astype(np.uint16)


def unstriped8(offs):
    return np.stack([offs[16 * g:16 * g + 16].T.reshape(-1) for g in range(8)]).astype(np.int64)


E2M1 = np.array([0.0, 0.5, 1.0, 1.5, 2.0, 3.0, 4.0, 6.0, -0.0, -0.5, -1.0, -1.5, -2.0, -3.0, -4.0, -6.0])


def pack_weight(w, fmt):
    k, n = w.shape
    w = f64(np.asarray(w, np.float32).astype(ml_dtypes.bfloat16)).reshape(k // 32, 32, n)
    amax = np.abs(w).max(1)
    if fmt == "e4m3":
        byte = np.frexp(amax)[1] - 1 + 127 - 7
    else:
        mant, ex = np.frexp(amax / 6.0)
        byte = np.where(mant > 0.5, ex, ex - 1) + 127
    byte = np.clip(np.where(amax > 0, byte, 1), 1, 254)
    scaled = (w * np.exp2(127.0 - byte)[:, None, :]).reshape(k, n).astype(np.float32)
    by_word = np.ascontiguousarray(scaled.reshape(k // 512, 128, 4, n).transpose(0, 1, 3, 2))
    if fmt == "e4m3":
        words = by_word.astype(ml_dtypes.float8_e4m3fn).view(np.uint8)
    else:
        c = by_word.astype(ml_dtypes.float4_e2m1fn).view(np.uint8) & 0xF
        words = (c[..., 0::2] | (c[..., 1::2] << 4)).reshape(k // 512, 128, 2 * n)
    return np.ascontiguousarray(words), np.ascontiguousarray(byte.astype(np.uint8).reshape(k // 512, 16, n))


def unpack_weight(words, scales, fmt):
    g, _, n = scales.shape
    words = np.ascontiguousarray(words).reshape(g, 128, n, -1)
    if fmt == "e4m3":
        vals = words.view(ml_dtypes.float8_e4m3fn).astype(np.float64)
    else:
        nib = np.empty((g, 128, n, 4), np.uint8)
        nib[..., 0::2] = words & 0xF
        nib[..., 1::2] = words >> 4
        vals = E2M1[nib]
    vals = vals * np.repeat(np.exp2(scales.astype(np.float64) - 127.0), 8, axis=1)[..., None]
    return vals.transpose(0, 1, 3, 2).reshape(g * 512, n)


def planes(y):
    n, m = y.shape
    v = y.astype(np.float32).astype(ml_dtypes.bfloat16).astype(np.float64).reshape(n // 32, 32, m)
    top = np.abs(v).max(1)
    byte = np.clip(np.where(top > 0, np.frexp(top)[1] - 1 + 127 - 7, 1), 1, 254)
    codes = (v * np.exp2(127.0 - byte)[:, None, :]).reshape(n, m).astype(np.float32).astype(ml_dtypes.float8_e4m3fn).view(np.uint8)
    words = codes.reshape(n // 512, 128, 4, m).transpose(0, 1, 3, 2)
    return np.ascontiguousarray(words), np.ascontiguousarray(byte.astype(np.uint8).reshape(n // 512, 16, m))


def silu(f):
    return f / (1.0 + np.exp(-np.maximum(f, -700.0)))


K, L, N, T, J = 1024, 512, 512, 2048, 1024


def setup_inputs():
    n = np.random.standard_normal
    s = mx_kscale(K)[:, None]
    s2 = mx_kscale(L)[:, None]
    p_wt4 = pack_weight(n((K, N)) / np.sqrt(K) / s, "e2m1")
    p_wx = pack_weight(n((L, N)) / np.sqrt(L) / s2, "e2m1")
    return {
        "xT": (n((K, T)) * s).astype(np.float32),
        "wgt": np.repeat(np.random.uniform(0.5, 2.0, (8, J)), 16, axis=0).astype(np.float32),
        "wt4_words": p_wt4[0],
        "wt4_scales": p_wt4[1],
        "wtd": (0.4 * (n((K, N)) / np.sqrt(K) / s)).astype(np.float32),
        "c": (n((L, J)) * s2).astype(np.float32),
        "wx_words": p_wx[0],
        "wx_scales": p_wx[1],
        "b": (0.3 * n(N)).astype(np.float32),
        "offs": striped8(np.stack([np.random.permutation(T)[:J] for _ in range(8)])),
    }


def reference(xT, wgt, wt4_words, wt4_scales, wtd, c, wx_words, wx_scales, b, offs):
    idx = unstriped8(offs)
    rows = np.arange(K)
    xg = f64(wgt)[rows // 4 % 128] * f64(xT)[rows[:, None], idx[rows % 512 // 64]]
    xT_ = mxq(xg, 0, "e4m3")
    wt4_ = unpack_weight(wt4_words, wt4_scales, "e2m1")
    wtd_ = mxq(f64(wtd), 0, "e4m3")
    c_q_ = mxq(f64(c), 0, "e4m3")
    c_r_ = mxq(f64(c) - c_q_, 0, "e4m3")
    wx_ = unpack_weight(wx_words, wx_scales, "e2m1")
    y = wt4_.T @ xT_ + wtd_.T @ xT_ + wx_.T @ c_q_ + wx_.T @ c_r_
    out_0 = silu(y + f64(b)[:, None])
    return (out_0,) + planes(out_0)

@@ -1,0 +1,273 @@
+from contextlib import ExitStack
+
+import concourse.mybir as mybir
+
+K, L, N, T, J = 1024, 512, 512, 2048, 1024
+FLOPS = 2 * N * J * (2 * K + 2 * L) + 2 * L * L * J
+
+F32 = mybir.dt.float32
+BF16 = mybir.dt.bfloat16
+I32 = mybir.dt.int32
+U32 = mybir.dt.uint32
+U16 = mybir.dt.uint16
+U8 = mybir.dt.uint8
+E4M3 = mybir.dt.float8_e4m3fn_x4
+E2M1 = mybir.dt.float4_e2m1fn_x4
+ALU = mybir.AluOpType
+ACT = mybir.ActivationFunctionType
+
+P = 128
+H = 512
+
+
+def tile_list_dl_siluP_kernel(
+    tc, xT, wgt, wt4_words, wt4_scales, wtd, c, wx_words, wx_scales, b, offs, out_0, out_1, out_2
+):
+    nc = tc.nc
+    with ExitStack() as ctx:
+        held = ctx.enter_context(tc.tile_pool(name="held", bufs=1))
+        stage = ctx.enter_context(tc.tile_pool(name="stage", bufs=6))
+        psum = ctx.enter_context(tc.psum_pool(name="psum", bufs=1))
+
+        def cols(h):
+            return slice(h * H, (h + 1) * H)
+
+        warm = held.tile([P, 8], F32, name="warm")
+        warm2 = held.tile([P, 8], F32, name="warm2")
+        nc.vector.memset(warm[:], 0.0)
+        nc.scalar.activation(warm2[:], warm[:], ACT.Silu)
+
+        raw_scales = held.tile([P, 3, N], U8, name="raw_scales", align_bytes=64)
+        nc.vector.memset(raw_scales[:].rearrange("p a n -> p (a n)").bitcast(I32), 0)
+        ident = held.tile([P, 4 * 512], BF16, name="ident", align_bytes=64)
+        seed = held.tile([P, 516], BF16, name="seed", align_bytes=64)
+        nc.vector.memset(seed[:], 0.0)
+        nc.gpsimd.affine_select(
+            out=seed[:], in_=seed[:], pattern=[[1, 516]],
+            compare_op=ALU.not_equal, fill=1.0, base=-3, channel_multiplier=-4,
+        )
+        for i in range(4):
+            nc.vector.tensor_copy(out=ident[:, i * 512 : (i + 1) * 512], in_=seed[:, 3 - i : 515 - i])
+        bias = held.tile([P, 4], F32, name="bias")
+
+        def load_scales(q):
+            nc.sync.dma_start(
+                out=raw_scales[32 * q : 32 * q + 4, 2, :].bitcast(I32),
+                in_=wx_scales[0, 4 * q : 4 * q + 4, :].bitcast(I32),
+            )
+            nc.sync.dma_start(
+                out=raw_scales[32 * q : 32 * q + 4, 0:2, :].bitcast(I32),
+                in_=wt4_scales[:, 4 * q : 4 * q + 4, :].rearrange("a r n -> r a n").bitcast(I32),
+            )
+
+        offsets = held.tile([P, J // 16], U16, name="offsets")
+        nc.sync.dma_start(offsets[:], offs)
+        raw_w4 = held.tile([P, 2, 2 * N], U8, name="raw_w4", align_bytes=64)
+        raw_wx = held.tile([P, 2 * N], U8, name="raw_wx", align_bytes=64)
+        nc.sync.dma_start(out=raw_w4[:].bitcast(I32), in_=wt4_words.rearrange("a p n -> p a n").bitcast(I32))
+        nc.sync.dma_start(out=raw_wx[:].bitcast(I32), in_=wx_words[0].bitcast(I32))
+        weight = held.tile([P, J], F32, name="weight")
+        x_rows = xT.rearrange("(a p i) t -> a i p t", a=2, i=4)
+        planes = [held.tile([P, T], F32, name="plane%d" % u) for u in range(8)]
+        c_raw = [held.tile([P, 4, H], F32, name="c_raw%d" % h) for h in range(2)]
+        wd_raw = [held.tile([P, 4, N], F32, name="wd_raw%d" % a) for a in range(2)]
+        c_rows = c.rearrange("(p i) j -> p i j", i=4)
+        wd_rows = wtd.rearrange("(a p i) n -> a p i n", a=2, i=4)
+
+        def load_x(u):
+            nc.sync.dma_start(out=planes[u][:], in_=x_rows[u // 4, u % 4])
+
+        def load_c(h):
+            nc.sync.dma_start(out=c_raw[h][:], in_=c_rows[:, :, cols(h)])
+
+        def load_wd(a):
+            nc.sync.dma_start(out=wd_raw[a][:], in_=wd_rows[a])
+
+        nc.sync.dma_start(out=weight[:, cols(0)], in_=wgt[:, cols(0)])
+        load_x(0)
+        nc.sync.dma_start(out=weight[:, cols(1)], in_=wgt[:, cols(1)])
+        load_c(0)
+        load_scales(0)
+        load_x(1)
+        load_scales(1)
+        load_wd(0)
+        load_scales(2)
+        load_x(2)
+        load_scales(3)
+        nc.sync.dma_start(out=bias[:], in_=b.rearrange("(p t) -> p t", t=4))
+        load_x(3)
+        load_c(1)
+        load_x(4)
+        load_wd(1)
+        load_x(5)
+        load_x(6)
+        load_x(7)
+
+        def quantise(src, name, width=H):
+            codes = held.tile([P, width], U32, name=name + "_codes", align_bytes=64)
+            scales = held.tile([P, width], U8, name=name + "_scales", align_bytes=64)
+            nc.vector.quantize_mx(out=codes[:].bitcast(E4M3), scales=scales[:], in_=src)
+            return codes, scales
+
+        def staged():
+            return stage.tile([P, 4 * H], BF16, name="staged", tag="staged", align_bytes=64)
+
+        def copy_on(engine, out, in_):
+            if engine == "vector":
+                nc.vector.tensor_copy(out=out, in_=in_)
+            else:
+                nc.scalar.copy(out=out, in_=in_)
+
+        def woven(dst):
+            return dst.rearrange("p (c e i) -> p c i e", e=4, i=4)
+
+        def by_plane(src):
+            return src.rearrange("p i (c e) -> p c i e", e=4)
+
+        w4 = held.tile([P, 2, 2 * N], U8, name="w4", align_bytes=64)
+        wx = held.tile([P, 2 * N], U8, name="wx", align_bytes=64)
+        nc.vector.tensor_copy(
+            out=w4[:].bitcast(U16).rearrange("p a (t m) -> p a m t", t=4),
+            in_=raw_w4[:].bitcast(U16).rearrange("p a (m t) -> p a m t", t=4),
+        )
+        nc.vector.tensor_copy(
+            out=wx[:].bitcast(U16).rearrange("p (t m) -> p m t", t=4),
+            in_=raw_wx[:].bitcast(U16).rearrange("p (m t) -> p m t", t=4),
+        )
+        id_codes, id_scales = quantise(ident[:], "ident")
+        fp4_scales = held.tile([P, 3, N], U8, name="fp4_scales", align_bytes=64)
+        nc.vector.tensor_copy(
+            out=fp4_scales[:].rearrange("p a (t m) -> p a m t", t=4),
+            in_=raw_scales[:].rearrange("p a (m t) -> p a m t", t=4),
+        )
+
+        picked = [held.tile([P, 4, J], F32, name="picked%d" % a) for a in range(2)]
+
+        def gather(u, part):
+            a, i = divmod(u, 4)
+            nc.vector.tensor_tensor(
+                picked[a][:, i, part],
+                planes[u][:].indirect(offsets[:, part.start // 16 : part.stop // 16]),
+                weight[:, part],
+                ALU.mult,
+            )
+
+        def bank(h, t):
+            return psum.tile([P, H], F32, name="bank", tag="bank%d%d" % (h, t))
+
+        cq, cr, xq, wd = {}, {}, {}, {}
+
+        def tiers(h):
+            rounded = staged()
+            copy_on("scalar", woven(rounded[:]), by_plane(c_raw[h][:]))
+            cq[h] = quantise(rounded[:], "cq%d" % h)
+            rest = staged()
+            for s in range(4):
+                part = slice(s * P, (s + 1) * P)
+                back = bank(1, s)
+                for i in range(4):
+                    nc.tensor.matmul_mx(
+                        out=back[:, i * P : (i + 1) * P],
+                        lhsT=id_codes[:, i * P : (i + 1) * P].bitcast(E4M3),
+                        lhsT_scale=id_scales[:, i * P : (i + 1) * P],
+                        rhs=cq[h][0][:, part].bitcast(E4M3),
+                        rhs_scale=cq[h][1][:, part],
+                        start=True, stop=True,
+                    )
+                nc.vector.tensor_tensor(
+                    woven(rest[:, s * 4 * P : (s + 1) * 4 * P]),
+                    by_plane(c_raw[h][:, :, part]),
+                    by_plane(back[:].rearrange("p (i j) -> p i j", i=4)),
+                    ALU.subtract,
+                )
+            cr[h] = quantise(rest[:], "cr%d" % h)
+
+        def change(a):
+            rounded = staged()
+            copy_on(
+                "scalar",
+                rounded[:].rearrange("p (t m i) -> p m i t", t=4, i=4),
+                wd_raw[a][:].rearrange("p i (m t) -> p m i t", t=4),
+            )
+            wd[a] = quantise(rounded[:], "wd%d" % a)
+
+        def picks(a, h, engine):
+            rounded = staged()
+            copy_on(engine, woven(rounded[:]), by_plane(picked[a][:, :, cols(h)]))
+            xq[a, h] = quantise(rounded[:], "xq%d%d" % (a, h))
+
+        acc = {}
+
+        def fp4_pass(h, t, words, plane, moving, start=False):
+            nc.tensor.matmul_mx(
+                out=acc[h, t][:],
+                lhsT=words[:, 2 * P * t : 2 * P * (t + 1)].bitcast(E2M1),
+                lhsT_scale=fp4_scales[:, plane, t * P : (t + 1) * P],
+                rhs=moving[0][:].bitcast(E4M3), rhs_scale=moving[1][:],
+                start=start, stop=False,
+            )
+
+        def fp8_pass(h, t, a, stop):
+            nc.tensor.matmul_mx(
+                out=acc[h, t][:],
+                lhsT=wd[a][0][:, t * P : (t + 1) * P].bitcast(E4M3),
+                lhsT_scale=wd[a][1][:, t * P : (t + 1) * P],
+                rhs=xq[a, h][0][:].bitcast(E4M3), rhs_scale=xq[a, h][1][:],
+                start=False, stop=stop,
+            )
+
+        def own_passes(h):
+            for t in range(4):
+                acc[h, t] = bank(h, t)
+                fp4_pass(h, t, wx[:], 2, cq[h], start=True)
+                fp4_pass(h, t, wx[:], 2, cr[h])
+
+        def pick_passes(a, h):
+            for t in range(4):
+                fp4_pass(h, t, w4[:, a, :], a, xq[a, h])
+                fp8_pass(h, t, a, stop=(a == 1))
+
+        whole = slice(0, J)
+        gather(0, cols(0))
+        gather(0, cols(1))
+        tiers(0)
+        own_passes(0)
+        gather(1, whole)
+        change(0)
+        gather(2, whole)
+        gather(3, whole)
+        picks(0, 0, "scalar")
+        pick_passes(0, 0)
+        tiers(1)
+        own_passes(1)
+        picks(0, 1, "scalar")
+        pick_passes(0, 1)
+        gather(4, whole)
+        change(1)
+        gather(5, whole)
+        gather(6, whole)
+        gather(7, cols(0))
+        gather(7, cols(1))
+        picks(1, 0, "scalar")
+        picks(1, 1, "vector")
+
+        y_rows = out_0.rearrange("(p t) j -> p t j", t=4)
+        y_words = out_1[0].rearrange("p j i -> p (j i)").bitcast(I32)
+        y_codes = held.tile([P, J], U32, name="y_codes", align_bytes=64)
+        y_scales = held.tile([P, J], U8, name="y_scales", align_bytes=64)
+        for h in range(2):
+            pick_passes(1, h)
+            y = held.tile([P, 4, H], F32, name="y%d" % h)
+            for t in range(4):
+                nc.scalar.activation(y[:, t, :], acc[h, t][:], ACT.Silu, bias=bias[:, t : t + 1])
+                nc.sync.dma_start(out=y_rows[:, t, cols(h)], in_=y[:, t, :])
+            rounded = staged()
+            copy_on("vector", woven(rounded[:]), by_plane(y[:]))
+            nc.vector.quantize_mx(out=y_codes[:, cols(h)].bitcast(E4M3), scales=y_scales[:, cols(h)], in_=rounded[:])
+            nc.sync.dma_start(out=y_words[:, cols(h)], in_=y_codes[:, cols(h)].bitcast(I32))
+        for q in range(4):
+            queue = nc.sync if q % 2 == 0 else nc.scalar
+            queue.dma_start(
+                out=out_2[0, 4 * q : 4 * q + 4, :].bitcast(I32),
+                in_=y_scales[32 * q : 32 * q + 4, :].bitcast(I32),
+            )

@@ -18,6 +18,11 @@ ACT = mybir.ActivationFunctionType
 
 P = 128
 H = 512
+Q = 256
+RUN = 4
+FIRST, SECOND = slice(0, H), slice(H, J)
+CHUNKS = {"A": slice(0, H), "B": slice(H, H + Q), "C": slice(H + Q, J)}
+BANKS = {"A": (0, 1, 2, 3), "B": (4, 4, 5, 5), "C": (6, 6, 7, 7)}
 
 
 def tile_list_dl_siluP_kernel(
@@ -29,18 +34,21 @@ def tile_list_dl_siluP_kernel(
         stage = ctx.enter_context(tc.tile_pool(name="stage", bufs=6))
         psum = ctx.enter_context(tc.psum_pool(name="psum", bufs=1))
 
-        def cols(h):
-            return slice(h * H, (h + 1) * H)
+        def keep(shape, dtype, name, tag=None):
+            return held.tile(shape, dtype, name=name, tag=tag or name, align_bytes=64)
 
-        warm = held.tile([P, 8], F32, name="warm")
-        warm2 = held.tile([P, 8], F32, name="warm2")
+        def width(part):
+            return part.stop - part.start
+
+        warm = keep([P, 8], F32, "warm")
+        warm2 = keep([P, 8], F32, "warm2")
         nc.vector.memset(warm[:], 0.0)
         nc.scalar.activation(warm2[:], warm[:], ACT.Silu)
 
-        raw_scales = held.tile([P, 3, N], U8, name="raw_scales", align_bytes=64)
+        raw_scales = keep([P, 3, N], U8, "raw_scales")
         nc.vector.memset(raw_scales[:].rearrange("p a n -> p (a n)").bitcast(I32), 0)
-        ident = held.tile([P, 4 * 512], BF16, name="ident", align_bytes=64)
-        seed = held.tile([P, 516], BF16, name="seed", align_bytes=64)
+        ident = keep([P, 4 * 512], BF16, "ident")
+        seed = keep([P, 516], BF16, "seed")
         nc.vector.memset(seed[:], 0.0)
         nc.gpsimd.affine_select(
             out=seed[:], in_=seed[:], pattern=[[1, 516]],
@@ -48,7 +56,30 @@ def tile_list_dl_siluP_kernel(
         )
         for i in range(4):
             nc.vector.tensor_copy(out=ident[:, i * 512 : (i + 1) * 512], in_=seed[:, 3 - i : 515 - i])
-        bias = held.tile([P, 4], F32, name="bias")
+        bias = keep([P, 4], F32, "bias")
+
+        offsets = held.tile([P, J // 16], U16, name="offsets")
+        nc.sync.dma_start(offsets[:], offs)
+        raw_w4 = keep([P, 2, 2 * N], U8, "raw_w4")
+        raw_wx = keep([P, 2 * N], U8, "raw_wx")
+        nc.sync.dma_start(out=raw_w4[:].bitcast(I32), in_=wt4_words.rearrange("a p n -> p a n").bitcast(I32))
+        nc.sync.dma_start(out=raw_wx[:].bitcast(I32), in_=wx_words[0].bitcast(I32))
+        weight = [keep([P, H], F32, "weight%d" % h) for h in range(2)]
+        x_rows = xT.rearrange("(a p i) t -> a i p t", a=2, i=4)
+        planes = [keep([P, T], F32, "plane%d" % u) for u in range(8)]
+        c_raw = [keep([P, 4, Q], F32, "c_raw%d" % q) for q in range(4)]
+        wd_raw = [keep([P, 4, N], F32, "wd_raw%d" % a) for a in range(2)]
+        c_rows = c.rearrange("(p i) j -> p i j", i=4)
+        wd_rows = wtd.rearrange("(a p i) n -> a p i n", a=2, i=4)
+
+        def load_x(u):
+            nc.sync.dma_start(out=planes[u][:], in_=x_rows[u // 4, u % 4])
+
+        def load_c(q):
+            nc.sync.dma_start(out=c_raw[q][:], in_=c_rows[:, :, q * Q : (q + 1) * Q])
+
+        def load_wd(a):
+            nc.sync.dma_start(out=wd_raw[a][:], in_=wd_rows[a])
 
         def load_scales(q):
             nc.sync.dma_start(
@@ -60,57 +91,36 @@ def tile_list_dl_siluP_kernel(
                 in_=wt4_scales[:, 4 * q : 4 * q + 4, :].rearrange("a r n -> r a n").bitcast(I32),
             )
 
-        offsets = held.tile([P, J // 16], U16, name="offsets")
-        nc.sync.dma_start(offsets[:], offs)
-        raw_w4 = held.tile([P, 2, 2 * N], U8, name="raw_w4", align_bytes=64)
-        raw_wx = held.tile([P, 2 * N], U8, name="raw_wx", align_bytes=64)
-        nc.sync.dma_start(out=raw_w4[:].bitcast(I32), in_=wt4_words.rearrange("a p n -> p a n").bitcast(I32))
-        nc.sync.dma_start(out=raw_wx[:].bitcast(I32), in_=wx_words[0].bitcast(I32))
-        weight = held.tile([P, J], F32, name="weight")
-        x_rows = xT.rearrange("(a p i) t -> a i p t", a=2, i=4)
-        planes = [held.tile([P, T], F32, name="plane%d" % u) for u in range(8)]
-        c_raw = [held.tile([P, 4, H], F32, name="c_raw%d" % h) for h in range(2)]
-        wd_raw = [held.tile([P, 4, N], F32, name="wd_raw%d" % a) for a in range(2)]
-        c_rows = c.rearrange("(p i) j -> p i j", i=4)
-        wd_rows = wtd.rearrange("(a p i) n -> a p i n", a=2, i=4)
-
-        def load_x(u):
-            nc.sync.dma_start(out=planes[u][:], in_=x_rows[u // 4, u % 4])
-
-        def load_c(h):
-            nc.sync.dma_start(out=c_raw[h][:], in_=c_rows[:, :, cols(h)])
-
-        def load_wd(a):
-            nc.sync.dma_start(out=wd_raw[a][:], in_=wd_rows[a])
-
-        nc.sync.dma_start(out=weight[:, cols(0)], in_=wgt[:, cols(0)])
-        load_x(0)
-        nc.sync.dma_start(out=weight[:, cols(1)], in_=wgt[:, cols(1)])
         load_c(0)
+        load_c(1)
+        nc.sync.dma_start(out=weight[0][:], in_=wgt[:, FIRST])
+        load_x(0)
+        nc.sync.dma_start(out=weight[1][:], in_=wgt[:, SECOND])
         load_scales(0)
         load_x(1)
         load_scales(1)
-        load_wd(0)
-        load_scales(2)
         load_x(2)
+        load_scales(2)
+        load_wd(0)
         load_scales(3)
-        nc.sync.dma_start(out=bias[:], in_=b.rearrange("(p t) -> p t", t=4))
+        load_c(2)
+        load_c(3)
         load_x(3)
-        load_c(1)
+        nc.sync.dma_start(out=bias[:], in_=b.rearrange("(p t) -> p t", t=4))
         load_x(4)
         load_wd(1)
         load_x(5)
         load_x(6)
         load_x(7)
 
-        def quantise(src, name, width=H):
-            codes = held.tile([P, width], U32, name=name + "_codes", align_bytes=64)
-            scales = held.tile([P, width], U8, name=name + "_scales", align_bytes=64)
-            nc.vector.quantize_mx(out=codes[:].bitcast(E4M3), scales=scales[:], in_=src)
-            return codes, scales
+        def operand(name):
+            return keep([P, J], U32, name + "_codes"), keep([P, J], U8, name + "_scales")
 
-        def staged():
-            return stage.tile([P, 4 * H], BF16, name="staged", tag="staged", align_bytes=64)
+        def quantise(dst, part, src):
+            nc.vector.quantize_mx(out=dst[0][:, part].bitcast(E4M3), scales=dst[1][:, part], in_=src)
+
+        def staged(columns):
+            return stage.tile([P, 4 * H], BF16, name="staged", tag="staged", align_bytes=64)[:, 0 : 4 * columns]
 
         def copy_on(engine, out, in_):
             if engine == "vector":
@@ -119,13 +129,16 @@ def tile_list_dl_siluP_kernel(
                 nc.scalar.copy(out=out, in_=in_)
 
         def woven(dst):
-            return dst.rearrange("p (c e i) -> p c i e", e=4, i=4)
+            return dst.rearrange("p (c e i) -> p c i e", e=RUN, i=4)
 
         def by_plane(src):
-            return src.rearrange("p i (c e) -> p c i e", e=4)
+            return src.rearrange("p i (c e) -> p c i e", e=RUN)
 
-        w4 = held.tile([P, 2, 2 * N], U8, name="w4", align_bytes=64)
-        wx = held.tile([P, 2 * N], U8, name="wx", align_bytes=64)
+        def four(flat):
+            return flat.rearrange("p (i j) -> p i j", i=4)
+
+        w4 = keep([P, 2, 2 * N], U8, "w4")
+        wx = keep([P, 2 * N], U8, "wx")
         nc.vector.tensor_copy(
             out=w4[:].bitcast(U16).rearrange("p a (t m) -> p a m t", t=4),
             in_=raw_w4[:].bitcast(U16).rearrange("p a (m t) -> p a m t", t=4),
@@ -134,140 +147,190 @@ def tile_list_dl_siluP_kernel(
             out=wx[:].bitcast(U16).rearrange("p (t m) -> p m t", t=4),
             in_=raw_wx[:].bitcast(U16).rearrange("p (m t) -> p m t", t=4),
         )
-        id_codes, id_scales = quantise(ident[:], "ident")
-        fp4_scales = held.tile([P, 3, N], U8, name="fp4_scales", align_bytes=64)
-        nc.vector.tensor_copy(
-            out=fp4_scales[:].rearrange("p a (t m) -> p a m t", t=4),
-            in_=raw_scales[:].rearrange("p a (m t) -> p a m t", t=4),
-        )
+        eye = keep([P, H], U32, "eye_codes"), keep([P, H], U8, "eye_scales")
+        quantise(eye, FIRST, ident[:])
 
-        picked = [held.tile([P, 4, J], F32, name="picked%d" % a) for a in range(2)]
+        cq = {0: (keep([P, H], U32, "cq0"), keep([P, H], U8, "cqs0"))}
+        cr = [(keep([P, H], U32, "cr%d" % h), keep([P, H], U8, "crs%d" % h)) for h in range(2)]
+        wd = {1: (keep([P, H], U32, "wd1"), keep([P, H], U8, "wds1"))}
+        xq = {(a, h): (keep([P, H], U32, "xq%d%d" % (a, h)), keep([P, H], U8, "xqs%d%d" % (a, h)))
+              for a in range(2) for h in range(2)}
 
-        def gather(u, part):
-            a, i = divmod(u, 4)
+        def gather(u, part, dst):
+            h = part.start // H
+            n = width(part)
+            i = u % 4
             nc.vector.tensor_tensor(
-                picked[a][:, i, part],
+                dst[:, i * n : (i + 1) * n],
                 planes[u][:].indirect(offsets[:, part.start // 16 : part.stop // 16]),
-                weight[:, part],
+                weight[h][:, part.start - h * H : part.stop - h * H],
                 ALU.mult,
             )
 
-        def bank(h, t):
-            return psum.tile([P, H], F32, name="bank", tag="bank%d%d" % (h, t))
+        def bank(n):
+            return psum.tile([P, H], F32, name="bank", tag="bank%d" % n)
 
-        cq, cr, xq, wd = {}, {}, {}, {}
+        def first_tier(q, engine, rounded):
+            copy_on(engine, woven(rounded), by_plane(c_raw[q][:]))
+            quantise(cq[q // 2], slice(q % 2 * Q, (q % 2 + 1) * Q), rounded)
 
-        def tiers(h):
-            rounded = staged()
-            copy_on("scalar", woven(rounded[:]), by_plane(c_raw[h][:]))
-            cq[h] = quantise(rounded[:], "cq%d" % h)
-            rest = staged()
+        def second_tier(h, rest):
             for s in range(4):
                 part = slice(s * P, (s + 1) * P)
-                back = bank(1, s)
+                back = bank(4 + s)
                 for i in range(4):
                     nc.tensor.matmul_mx(
                         out=back[:, i * P : (i + 1) * P],
-                        lhsT=id_codes[:, i * P : (i + 1) * P].bitcast(E4M3),
-                        lhsT_scale=id_scales[:, i * P : (i + 1) * P],
+                        lhsT=eye[0][:, i * P : (i + 1) * P].bitcast(E4M3),
+                        lhsT_scale=eye[1][:, i * P : (i + 1) * P],
                         rhs=cq[h][0][:, part].bitcast(E4M3),
                         rhs_scale=cq[h][1][:, part],
                         start=True, stop=True,
                     )
                 nc.vector.tensor_tensor(
                     woven(rest[:, s * 4 * P : (s + 1) * 4 * P]),
-                    by_plane(c_raw[h][:, :, part]),
-                    by_plane(back[:].rearrange("p (i j) -> p i j", i=4)),
+                    by_plane(c_raw[2 * h + s // 2][:, :, s % 2 * P : (s % 2 + 1) * P]),
+                    by_plane(four(back[:])),
                     ALU.subtract,
                 )
-            cr[h] = quantise(rest[:], "cr%d" % h)
+            quantise(cr[h], FIRST, rest)
 
-        def change(a):
-            rounded = staged()
+        def change(a, rounded):
             copy_on(
                 "scalar",
-                rounded[:].rearrange("p (t m i) -> p m i t", t=4, i=4),
+                rounded.rearrange("p (t m i) -> p m i t", t=4, i=4),
                 wd_raw[a][:].rearrange("p i (m t) -> p m i t", t=4),
             )
-            wd[a] = quantise(rounded[:], "wd%d" % a)
+            quantise(wd[a], FIRST, rounded)
 
-        def picks(a, h, engine):
-            rounded = staged()
-            copy_on(engine, woven(rounded[:]), by_plane(picked[a][:, :, cols(h)]))
-            xq[a, h] = quantise(rounded[:], "xq%d%d" % (a, h))
+        def local(part):
+            return slice(part.start % H, (part.stop - 1) % H + 1)
+
+        def picks(a, part, src, engine, rounded):
+            copy_on(engine, woven(rounded), by_plane(four(src)))
+            quantise(xq[a, part.start // H], local(part), rounded)
 
         acc = {}
 
-        def fp4_pass(h, t, words, plane, moving, start=False):
-            nc.tensor.matmul_mx(
-                out=acc[h, t][:],
-                lhsT=words[:, 2 * P * t : 2 * P * (t + 1)].bitcast(E2M1),
-                lhsT_scale=fp4_scales[:, plane, t * P : (t + 1) * P],
-                rhs=moving[0][:].bitcast(E4M3), rhs_scale=moving[1][:],
-                start=start, stop=False,
-            )
-
-        def fp8_pass(h, t, a, stop):
-            nc.tensor.matmul_mx(
-                out=acc[h, t][:],
-                lhsT=wd[a][0][:, t * P : (t + 1) * P].bitcast(E4M3),
-                lhsT_scale=wd[a][1][:, t * P : (t + 1) * P],
-                rhs=xq[a, h][0][:].bitcast(E4M3), rhs_scale=xq[a, h][1][:],
-                start=False, stop=stop,
-            )
-
-        def own_passes(h):
+        def open_chunk(name):
+            tiles = {n: bank(n) for n in sorted(set(BANKS[name]))}
+            n = width(CHUNKS[name])
             for t in range(4):
-                acc[h, t] = bank(h, t)
-                fp4_pass(h, t, wx[:], 2, cq[h], start=True)
-                fp4_pass(h, t, wx[:], 2, cr[h])
+                at = (t * n) % H
+                acc[name, t] = tiles[BANKS[name][t]][:, at : at + n]
 
-        def pick_passes(a, h):
+        def mx_pass(name, t, fixed, fixed_scale, moving, step, start=False, stop=False):
+            part = local(CHUNKS[name])
+            starts = list(range(0, width(part), step))
+            for at in starts:
+                cols = slice(part.start + at, part.start + at + step)
+                nc.tensor.matmul_mx(
+                    out=acc[name, t][:, at : at + step], lhsT=fixed, lhsT_scale=fixed_scale,
+                    rhs=moving[0][:, cols].bitcast(E4M3), rhs_scale=moving[1][:, cols],
+                    start=start and at == starts[0], stop=stop and at == starts[-1],
+                )
+
+        def fp4_pass(name, t, words, plane, moving, start=False):
+            mx_pass(name, t, words[:, 2 * P * t : 2 * P * (t + 1)].bitcast(E2M1),
+                    fp4_scales[:, plane, t * P : (t + 1) * P], moving, H if name == "A" else P, start=start)
+
+        def own_passes(name):
+            open_chunk(name)
+            h = CHUNKS[name].start // H
             for t in range(4):
-                fp4_pass(h, t, w4[:, a, :], a, xq[a, h])
-                fp8_pass(h, t, a, stop=(a == 1))
+                opens = t == 0 or BANKS[name][t] != BANKS[name][t - 1]
+                fp4_pass(name, t, wx[:], 2, cq[h], start=opens)
+                fp4_pass(name, t, wx[:], 2, cr[h])
 
-        whole = slice(0, J)
-        gather(0, cols(0))
-        gather(0, cols(1))
-        tiers(0)
-        own_passes(0)
-        gather(1, whole)
-        change(0)
-        gather(2, whole)
-        gather(3, whole)
-        picks(0, 0, "scalar")
-        pick_passes(0, 0)
-        tiers(1)
-        own_passes(1)
-        picks(0, 1, "scalar")
-        pick_passes(0, 1)
-        gather(4, whole)
-        change(1)
-        gather(5, whole)
-        gather(6, whole)
-        gather(7, cols(0))
-        gather(7, cols(1))
-        picks(1, 0, "scalar")
-        picks(1, 1, "vector")
+        def pick_passes(a, name):
+            moving = xq[a, CHUNKS[name].start // H]
+            for t in range(4):
+                closes = a == 1 and (t == 3 or BANKS[name][t] != BANKS[name][t + 1])
+                fp4_pass(name, t, w4[:, a, :], a, moving)
+                mx_pass(name, t, wd[a][0][:, t * P : (t + 1) * P].bitcast(E4M3), wd[a][1][:, t * P : (t + 1) * P],
+                        moving, width(CHUNKS[name]), stop=closes)
 
         y_rows = out_0.rearrange("(p t) j -> p t j", t=4)
         y_words = out_1[0].rearrange("p j i -> p (j i)").bitcast(I32)
-        y_codes = held.tile([P, J], U32, name="y_codes", align_bytes=64)
-        y_scales = held.tile([P, J], U8, name="y_scales", align_bytes=64)
-        for h in range(2):
-            pick_passes(1, h)
-            y = held.tile([P, 4, H], F32, name="y%d" % h)
+        y_mx = operand("y")
+        y = {name: keep([P, 4, width(part)], F32, "y" + name) for name, part in CHUNKS.items()}
+
+        def finish(name):
+            part = CHUNKS[name]
             for t in range(4):
-                nc.scalar.activation(y[:, t, :], acc[h, t][:], ACT.Silu, bias=bias[:, t : t + 1])
-                nc.sync.dma_start(out=y_rows[:, t, cols(h)], in_=y[:, t, :])
-            rounded = staged()
-            copy_on("vector", woven(rounded[:]), by_plane(y[:]))
-            nc.vector.quantize_mx(out=y_codes[:, cols(h)].bitcast(E4M3), scales=y_scales[:, cols(h)], in_=rounded[:])
-            nc.sync.dma_start(out=y_words[:, cols(h)], in_=y_codes[:, cols(h)].bitcast(I32))
+                nc.scalar.activation(y[name][:, t, :], acc[name, t], ACT.Silu, bias=bias[:, t : t + 1])
+                if name == "A":
+                    nc.sync.dma_start(out=y_rows[:, t, part], in_=y[name][:, t, :])
+                elif t % 2 == 1:
+                    nc.sync.dma_start(out=y_rows[:, t - 1 : t + 1, part], in_=y[name][:, t - 1 : t + 1, :])
+
+        def hand_on(name, engine):
+            part = CHUNKS[name]
+            rounded = staged(width(part))
+            copy_on(engine, woven(rounded), by_plane(y[name][:]))
+            quantise(y_mx, part, rounded)
+            nc.sync.dma_start(out=y_words[:, part], in_=y_mx[0][:, part].bitcast(I32))
+
+        first_tier(0, "vector", staged(Q))
+        first_tier(1, "scalar", staged(Q))
+        second_tier(0, keep([P, 4 * H], BF16, "rest0", tag="low0")[:])
+        low = [keep([P, 4 * H], F32, "low0"), keep([P, 4 * H], F32, "low1", tag="c_raw1")]
+        for u in range(2):
+            gather(u, FIRST, low[0])
+            gather(u, SECOND, low[1])
+        fp4_scales = keep([P, 3, N], U8, "fp4_scales", tag="plane1")
+        nc.vector.tensor_copy(
+            out=fp4_scales[:].rearrange("p a (t m) -> p a m t", t=4),
+            in_=raw_scales[:].rearrange("p a (m t) -> p a m t", t=4),
+        )
+        own_passes("A")
+        gather(2, FIRST, low[0])
+        gather(2, SECOND, low[1])
+        pair = keep([P, 2 * H], U32, "pair", tag="plane2")
+        wd[0] = pair[:, 0:H], keep([P, H], U8, "wds0")
+        cq[1] = pair[:, H : 2 * H], keep([P, H], U8, "cqs1")
+        change(0, staged(H))
+        for h in range(2):
+            first_tier(2 + h, "scalar", low[h][:, 3 * H : 4 * H].bitcast(BF16))
+        gather(3, FIRST, low[0])
+        gather(3, SECOND, low[1])
+        second_tier(1, keep([P, 4 * H], BF16, "rest1", tag="plane3")[:])
+        high_a = keep([P, 4 * H], F32, "high_a", tag="plane3")
+        gather(4, FIRST, high_a)
+        picks(0, FIRST, low[0][:], "scalar", staged(H))
+        pick_passes(0, "A")
+        own_passes("B")
+        own_passes("C")
+        picks(0, SECOND, low[1][:], "scalar", staged(H))
+        pick_passes(0, "B")
+        pick_passes(0, "C")
+        gather(5, FIRST, high_a)
+        change(1, keep([P, 4 * H], BF16, "rounded_wd1", tag="c_raw1")[:])
+        gather(6, FIRST, high_a)
+        gather(7, FIRST, high_a)
+        high_b = keep([P, 4 * Q], F32, "high_b", tag="weight0")
+        for u in range(4, 8):
+            gather(u, CHUNKS["B"], high_b)
+        picks(1, FIRST, high_a[:], "scalar", keep([P, 4 * H], BF16, "rounded_a", tag="late")[:])
+        pick_passes(1, "A")
+        high_c = keep([P, 4 * Q], F32, "high_c", tag="late")
+        gather(4, CHUNKS["C"], high_c)
+        gather(5, CHUNKS["C"], high_c)
+        picks(1, CHUNKS["B"], high_b[:], "scalar", high_c[:, 2 * Q : 4 * Q].bitcast(BF16))
+        gather(6, CHUNKS["C"], high_c)
+        gather(7, CHUNKS["C"], high_c)
+        finish("A")
+        pick_passes(1, "B")
+        picks(1, CHUNKS["C"], high_c[:], "vector", staged(Q))
+        pick_passes(1, "C")
+        hand_on("A", "vector")
+        finish("B")
+        finish("C")
+        hand_on("C", "vector")
+        hand_on("B", "scalar")
         for q in range(4):
             queue = nc.sync if q % 2 == 0 else nc.scalar
             queue.dma_start(
                 out=out_2[0, 4 * q : 4 * q + 4, :].bitcast(I32),
-                in_=y_scales[32 * q : 32 * q + 4, :].bitcast(I32),
+                in_=y_mx[1][32 * q : 32 * q + 4, :].bitcast(I32),
             )

@@ -19,7 +19,7 @@ ACT = mybir.ActivationFunctionType
 P = 128
 H = 512
 Q = 256
-RUN = 4
+RUN = 2
 FIRST, SECOND = slice(0, H), slice(H, J)
 CHUNKS = {"A": slice(0, H), "B": slice(H, H + Q), "C": slice(H + Q, J)}
 BANKS = {"A": (0, 1, 2, 3), "B": (4, 4, 5, 5), "C": (6, 6, 7, 7)}
@@ -49,7 +49,7 @@ def tile_list_dl_siluP_kernel(
         nc.vector.memset(raw_scales[:].rearrange("p a n -> p (a n)").bitcast(I32), 0)
         ident = keep([P, 4 * 512], BF16, "ident")
         seed = keep([P, 516], BF16, "seed")
-        nc.vector.memset(seed[:], 0.0)
+        nc.gpsimd.memset(seed[:], 0.0)
         nc.gpsimd.affine_select(
             out=seed[:], in_=seed[:], pattern=[[1, 516]],
             compare_op=ALU.not_equal, fill=1.0, base=-3, channel_multiplier=-4,
@@ -60,14 +60,12 @@ def tile_list_dl_siluP_kernel(
 
         offsets = held.tile([P, J // 16], U16, name="offsets")
         nc.sync.dma_start(offsets[:], offs)
-        raw_w4 = keep([P, 2, 2 * N], U8, "raw_w4")
-        raw_wx = keep([P, 2 * N], U8, "raw_wx")
-        nc.sync.dma_start(out=raw_w4[:].bitcast(I32), in_=wt4_words.rearrange("a p n -> p a n").bitcast(I32))
-        nc.sync.dma_start(out=raw_wx[:].bitcast(I32), in_=wx_words[0].bitcast(I32))
-        weight = [keep([P, H], F32, "weight%d" % h) for h in range(2)]
+        raw_words = keep([P, 3, 2 * N], U8, "raw_words")
+        weight = keep([P, J], F32, "weight")
         x_rows = xT.rearrange("(a p i) t -> a i p t", a=2, i=4)
         planes = [keep([P, T], F32, "plane%d" % u) for u in range(8)]
-        c_raw = [keep([P, 4, Q], F32, "c_raw%d" % q) for q in range(4)]
+        c_parts = [slice(0, Q), slice(Q, H), SECOND]
+        c_raw = [keep([P, 4, width(part)], F32, "c_raw%d" % q) for q, part in enumerate(c_parts)]
         wd_raw = [keep([P, 4, N], F32, "wd_raw%d" % a) for a in range(2)]
         c_rows = c.rearrange("(p i) j -> p i j", i=4)
         wd_rows = wtd.rearrange("(a p i) n -> a p i n", a=2, i=4)
@@ -76,7 +74,7 @@ def tile_list_dl_siluP_kernel(
             nc.sync.dma_start(out=planes[u][:], in_=x_rows[u // 4, u % 4])
 
         def load_c(q):
-            nc.sync.dma_start(out=c_raw[q][:], in_=c_rows[:, :, q * Q : (q + 1) * Q])
+            nc.sync.dma_start(out=c_raw[q][:], in_=c_rows[:, :, c_parts[q]])
 
         def load_wd(a):
             nc.sync.dma_start(out=wd_raw[a][:], in_=wd_rows[a])
@@ -93,25 +91,24 @@ def tile_list_dl_siluP_kernel(
 
         load_c(0)
         load_c(1)
-        nc.sync.dma_start(out=weight[0][:], in_=wgt[:, FIRST])
+        nc.sync.dma_start(out=raw_words[:, 0:2, :].bitcast(I32), in_=wt4_words.rearrange("a p n -> p a n").bitcast(I32))
+        nc.sync.dma_start(out=raw_words[:, 2, :].bitcast(I32), in_=wx_words[0].bitcast(I32))
+        nc.sync.dma_start(out=weight[:], in_=wgt)
         load_x(0)
-        nc.sync.dma_start(out=weight[1][:], in_=wgt[:, SECOND])
         load_scales(0)
         load_x(1)
         load_scales(1)
         load_x(2)
         load_scales(2)
-        load_wd(0)
+        load_x(3)
         load_scales(3)
         load_c(2)
-        load_c(3)
-        load_x(3)
+        load_wd(0)
         nc.sync.dma_start(out=bias[:], in_=b.rearrange("(p t) -> p t", t=4))
         load_x(4)
         load_wd(1)
-        load_x(5)
-        load_x(6)
-        load_x(7)
+        for u in range(5, 8):
+            load_x(u)
 
         def operand(name):
             return keep([P, J], U32, name + "_codes"), keep([P, J], U8, name + "_scales")
@@ -137,33 +134,22 @@ def tile_list_dl_siluP_kernel(
         def four(flat):
             return flat.rearrange("p (i j) -> p i j", i=4)
 
-        w4 = keep([P, 2, 2 * N], U8, "w4")
-        wx = keep([P, 2 * N], U8, "wx")
-        nc.vector.tensor_copy(
-            out=w4[:].bitcast(U16).rearrange("p a (t m) -> p a m t", t=4),
-            in_=raw_w4[:].bitcast(U16).rearrange("p a (m t) -> p a m t", t=4),
-        )
-        nc.vector.tensor_copy(
-            out=wx[:].bitcast(U16).rearrange("p (t m) -> p m t", t=4),
-            in_=raw_wx[:].bitcast(U16).rearrange("p (m t) -> p m t", t=4),
-        )
         eye = keep([P, H], U32, "eye_codes"), keep([P, H], U8, "eye_scales")
         quantise(eye, FIRST, ident[:])
 
         cq = {0: (keep([P, H], U32, "cq0"), keep([P, H], U8, "cqs0"))}
         cr = [(keep([P, H], U32, "cr%d" % h), keep([P, H], U8, "crs%d" % h)) for h in range(2)]
-        wd = {1: (keep([P, H], U32, "wd1"), keep([P, H], U8, "wds1"))}
+        wd = {0: (keep([P, H], U32, "wd0"), keep([P, H], U8, "wds0")), 1: (keep([P, H], U32, "wd1"), keep([P, H], U8, "wds1"))}
         xq = {(a, h): (keep([P, H], U32, "xq%d%d" % (a, h)), keep([P, H], U8, "xqs%d%d" % (a, h)))
               for a in range(2) for h in range(2)}
 
         def gather(u, part, dst):
-            h = part.start // H
             n = width(part)
             i = u % 4
             nc.vector.tensor_tensor(
                 dst[:, i * n : (i + 1) * n],
                 planes[u][:].indirect(offsets[:, part.start // 16 : part.stop // 16]),
-                weight[h][:, part.start - h * H : part.stop - h * H],
+                weight[:, part],
                 ALU.mult,
             )
 
@@ -172,7 +158,7 @@ def tile_list_dl_siluP_kernel(
 
         def first_tier(q, engine, rounded):
             copy_on(engine, woven(rounded), by_plane(c_raw[q][:]))
-            quantise(cq[q // 2], slice(q % 2 * Q, (q % 2 + 1) * Q), rounded)
+            quantise(cq[q // 2], local(c_parts[q]), rounded)
 
         def second_tier(h, rest):
             for s in range(4):
@@ -189,7 +175,7 @@ def tile_list_dl_siluP_kernel(
                     )
                 nc.vector.tensor_tensor(
                     woven(rest[:, s * 4 * P : (s + 1) * 4 * P]),
-                    by_plane(c_raw[2 * h + s // 2][:, :, s % 2 * P : (s % 2 + 1) * P]),
+                    by_plane(c_raw[2][:, :, part] if h else c_raw[s // 2][:, :, s % 2 * P : (s % 2 + 1) * P]),
                     by_plane(four(back[:])),
                     ALU.subtract,
                 )
@@ -198,8 +184,8 @@ def tile_list_dl_siluP_kernel(
         def change(a, rounded):
             copy_on(
                 "scalar",
-                rounded.rearrange("p (t m i) -> p m i t", t=4, i=4),
-                wd_raw[a][:].rearrange("p i (m t) -> p m i t", t=4),
+                rounded.rearrange("p (s t m i) -> p s m i t", s=2, t=2, i=4),
+                wd_raw[a][:].rearrange("p i (m s t) -> p s m i t", s=2, t=2),
             )
             quantise(wd[a], FIRST, rounded)
 
@@ -207,7 +193,7 @@ def tile_list_dl_siluP_kernel(
             return slice(part.start % H, (part.stop - 1) % H + 1)
 
         def picks(a, part, src, engine, rounded):
-            copy_on(engine, woven(rounded), by_plane(four(src)))
+            copy_on(engine, woven(rounded), by_plane(src))
             quantise(xq[a, part.start // H], local(part), rounded)
 
         acc = {}
@@ -239,14 +225,14 @@ def tile_list_dl_siluP_kernel(
             h = CHUNKS[name].start // H
             for t in range(4):
                 opens = t == 0 or BANKS[name][t] != BANKS[name][t - 1]
-                fp4_pass(name, t, wx[:], 2, cq[h], start=opens)
-                fp4_pass(name, t, wx[:], 2, cr[h])
+                fp4_pass(name, t, fp4_words[:, 2, :], 2, cq[h], start=opens)
+                fp4_pass(name, t, fp4_words[:, 2, :], 2, cr[h])
 
         def pick_passes(a, name):
             moving = xq[a, CHUNKS[name].start // H]
             for t in range(4):
                 closes = a == 1 and (t == 3 or BANKS[name][t] != BANKS[name][t + 1])
-                fp4_pass(name, t, w4[:, a, :], a, moving)
+                fp4_pass(name, t, fp4_words[:, a, :], a, moving)
                 mx_pass(name, t, wd[a][0][:, t * P : (t + 1) * P].bitcast(E4M3), wd[a][1][:, t * P : (t + 1) * P],
                         moving, width(CHUNKS[name]), stop=closes)
 
@@ -271,57 +257,57 @@ def tile_list_dl_siluP_kernel(
             quantise(y_mx, part, rounded)
             nc.sync.dma_start(out=y_words[:, part], in_=y_mx[0][:, part].bitcast(I32))
 
-        first_tier(0, "vector", staged(Q))
-        first_tier(1, "scalar", staged(Q))
-        second_tier(0, keep([P, 4 * H], BF16, "rest0", tag="low0")[:])
-        low = [keep([P, 4 * H], F32, "low0"), keep([P, 4 * H], F32, "low1", tag="c_raw1")]
-        for u in range(2):
-            gather(u, FIRST, low[0])
-            gather(u, SECOND, low[1])
-        fp4_scales = keep([P, 3, N], U8, "fp4_scales", tag="plane1")
+        whole = slice(0, J)
+        rounded_c = keep([P, 4 * H], BF16, "rounded_c", tag="ident")
+        first_tier(0, "vector", rounded_c[:, 0 : 4 * Q])
+        first_tier(1, "vector", rounded_c[:, 4 * Q : 4 * H])
+        fp4_words = keep([P, 3, 2 * N], U8, "fp4_words", tag="ident")
         nc.vector.tensor_copy(
-            out=fp4_scales[:].rearrange("p a (t m) -> p a m t", t=4),
-            in_=raw_scales[:].rearrange("p a (m t) -> p a m t", t=4),
+            out=fp4_words[:].bitcast(U16).rearrange("p a (t m) -> p t a m", t=4),
+            in_=raw_words[:].bitcast(U16).rearrange("p a (m t) -> p t a m", t=4),
         )
-        own_passes("A")
-        gather(2, FIRST, low[0])
-        gather(2, SECOND, low[1])
-        pair = keep([P, 2 * H], U32, "pair", tag="plane2")
-        wd[0] = pair[:, 0:H], keep([P, H], U8, "wds0")
-        cq[1] = pair[:, H : 2 * H], keep([P, H], U8, "cqs1")
-        change(0, staged(H))
-        for h in range(2):
-            first_tier(2 + h, "scalar", low[h][:, 3 * H : 4 * H].bitcast(BF16))
-        gather(3, FIRST, low[0])
-        gather(3, SECOND, low[1])
-        second_tier(1, keep([P, 4 * H], BF16, "rest1", tag="plane3")[:])
-        high_a = keep([P, 4 * H], F32, "high_a", tag="plane3")
+        second_tier(0, keep([P, 4 * H], BF16, "rest0", tag="low")[:])
+        low = keep([P, 4 * J], F32, "low")
+        for u in range(4):
+            gather(u, whole, low)
+        spent = keep([P, 4 * H + 3 * N], U8, "spent", tag="plane3")
+        cq[1] = spent[:, 0 : 4 * H].bitcast(U32), keep([P, H], U8, "cqs1")
+        first_tier(2, "scalar", keep([P, 4 * H], BF16, "rounded_c2", tag="high_a")[:])
+        fp4_scales = spent[:, 4 * H : 4 * H + 3 * N].rearrange("p (a n) -> p a n", a=3)
+        nc.vector.tensor_copy(
+            out=fp4_scales.rearrange("p a (t m) -> p t a m", t=4),
+            in_=raw_scales[:].rearrange("p a (m t) -> p t a m", t=4),
+        )
+        high_a = keep([P, 7 * H], F32, "high_a")
         gather(4, FIRST, high_a)
-        picks(0, FIRST, low[0][:], "scalar", staged(H))
-        pick_passes(0, "A")
+        second_tier(1, high_a[:, H : 3 * H].bitcast(BF16))
+        own_passes("A")
         own_passes("B")
         own_passes("C")
-        picks(0, SECOND, low[1][:], "scalar", staged(H))
+        change(0, high_a[:, 5 * H : 7 * H].bitcast(BF16))
+        change(1, keep([P, 4 * H], BF16, "rounded_wd1", tag="wd_raw0")[:])
+        gather(5, FIRST, high_a)
+        picks(0, FIRST, four(low[:])[:, :, FIRST], "scalar", keep([P, 4 * H], BF16, "rounded_low", tag="wd_raw1")[:])
+        pick_passes(0, "A")
+        gather(6, FIRST, high_a)
+        picks(0, SECOND, four(low[:])[:, :, SECOND], "scalar", high_a[:, 3 * H : 5 * H].bitcast(BF16))
         pick_passes(0, "B")
         pick_passes(0, "C")
-        gather(5, FIRST, high_a)
-        change(1, keep([P, 4 * H], BF16, "rounded_wd1", tag="c_raw1")[:])
-        gather(6, FIRST, high_a)
         gather(7, FIRST, high_a)
-        high_b = keep([P, 4 * Q], F32, "high_b", tag="weight0")
+        high_b = keep([P, 4 * Q], F32, "high_b", tag="low")
         for u in range(4, 8):
             gather(u, CHUNKS["B"], high_b)
-        picks(1, FIRST, high_a[:], "scalar", keep([P, 4 * H], BF16, "rounded_a", tag="late")[:])
+        picks(1, FIRST, four(high_a[:, 0 : 4 * H]), "scalar", keep([P, 4 * H], BF16, "rounded_a", tag="late")[:])
         pick_passes(1, "A")
         high_c = keep([P, 4 * Q], F32, "high_c", tag="late")
         gather(4, CHUNKS["C"], high_c)
         gather(5, CHUNKS["C"], high_c)
-        picks(1, CHUNKS["B"], high_b[:], "scalar", high_c[:, 2 * Q : 4 * Q].bitcast(BF16))
+        picks(1, CHUNKS["B"], four(high_b[:]), "scalar", high_c[:, 2 * Q : 4 * Q].bitcast(BF16))
         gather(6, CHUNKS["C"], high_c)
         gather(7, CHUNKS["C"], high_c)
         finish("A")
         pick_passes(1, "B")
-        picks(1, CHUNKS["C"], high_c[:], "vector", staged(Q))
+        picks(1, CHUNKS["C"], four(high_c[:]), "vector", staged(Q))
         pick_passes(1, "C")
         hand_on("A", "vector")
         finish("B")

@@ -17,12 +17,39 @@ ALU = mybir.AluOpType
 ACT = mybir.ActivationFunctionType
 
 P = 128
-H = 512
-Q = 256
-RUN = 2
-FIRST, SECOND = slice(0, H), slice(H, J)
+PACK = 4
+H = J // 2
+Q = J // 4
+HALVES = (slice(0, H), slice(H, J))
 CHUNKS = {"A": slice(0, H), "B": slice(H, H + Q), "C": slice(H + Q, J)}
 BANKS = {"A": (0, 1, 2, 3), "B": (4, 4, 5, 5), "C": (6, 6, 7, 7)}
+FP4_STEP = {"A": H, "B": P, "C": P}
+C_PARTS = (slice(0, Q), slice(Q, H), slice(H, J))
+STAGING_BUFS = 5
+
+
+def width(part):
+    return part.stop - part.start
+
+
+def in_half(part):
+    return slice(part.start % H, (part.stop - 1) % H + 1)
+
+
+def block(n):
+    return slice(n * P, (n + 1) * P)
+
+
+def woven(dst):
+    return dst.rearrange("p (c e i) -> p c i e", e=2, i=PACK)
+
+
+def by_row(src):
+    return src.rearrange("p i (c e) -> p c i e", e=2)
+
+
+def four_rows(flat):
+    return flat.rearrange("p (i j) -> p i j", i=PACK)
 
 
 def tile_list_dl_siluP_kernel(
@@ -31,292 +58,263 @@ def tile_list_dl_siluP_kernel(
     nc = tc.nc
     with ExitStack() as ctx:
         held = ctx.enter_context(tc.tile_pool(name="held", bufs=1))
-        stage = ctx.enter_context(tc.tile_pool(name="stage", bufs=6))
+        stage = ctx.enter_context(tc.tile_pool(name="stage", bufs=STAGING_BUFS))
         psum = ctx.enter_context(tc.psum_pool(name="psum", bufs=1))
 
         def keep(shape, dtype, name, tag=None):
             return held.tile(shape, dtype, name=name, tag=tag or name, align_bytes=64)
 
-        def width(part):
-            return part.stop - part.start
+        def staged(columns):
+            return stage.tile([P, PACK * H], BF16, name="staged", tag="staged", align_bytes=64)[:, 0 : PACK * columns]
 
-        warm = keep([P, 8], F32, "warm")
-        warm2 = keep([P, 8], F32, "warm2")
-        nc.vector.memset(warm[:], 0.0)
-        nc.scalar.activation(warm2[:], warm[:], ACT.Silu)
+        def staged_in(tag, name):
+            return keep([P, PACK * H], BF16, name, tag=tag)[:]
+
+        def operand(name, columns=H):
+            return keep([P, columns], U32, name + "_codes"), keep([P, columns], U8, name + "_scales")
+
+        def bank(n):
+            return psum.tile([P, H], F32, name="bank", tag="bank%d" % n)
+
+        def quantise(dst, part, src):
+            nc.vector.quantize_mx(out=dst[0][:, part].bitcast(E4M3), scales=dst[1][:, part], in_=src)
+
+        def round_on(engine, out, in_):
+            if engine == "vector":
+                nc.vector.tensor_copy(out=out, in_=in_)
+            else:
+                nc.scalar.copy(out=out, in_=in_)
 
         raw_scales = keep([P, 3, N], U8, "raw_scales")
         nc.vector.memset(raw_scales[:].rearrange("p a n -> p (a n)").bitcast(I32), 0)
-        ident = keep([P, 4 * 512], BF16, "ident")
-        seed = keep([P, 516], BF16, "seed")
+
+        seed = keep([P, L + PACK], BF16, "seed")
         nc.gpsimd.memset(seed[:], 0.0)
         nc.gpsimd.affine_select(
-            out=seed[:], in_=seed[:], pattern=[[1, 516]],
-            compare_op=ALU.not_equal, fill=1.0, base=-3, channel_multiplier=-4,
+            out=seed[:], in_=seed[:], pattern=[[1, L + PACK]],
+            compare_op=ALU.not_equal, fill=1.0, base=1 - PACK, channel_multiplier=-PACK,
         )
-        for i in range(4):
-            nc.vector.tensor_copy(out=ident[:, i * 512 : (i + 1) * 512], in_=seed[:, 3 - i : 515 - i])
-        bias = keep([P, 4], F32, "bias")
+        ident = keep([P, PACK * L], BF16, "ident")
+        for i in range(PACK):
+            nc.vector.tensor_copy(out=ident[:, i * L : (i + 1) * L], in_=seed[:, PACK - 1 - i : PACK - 1 - i + L])
+        eye = operand("eye")
+        quantise(eye, slice(0, L), ident[:])
 
         offsets = held.tile([P, J // 16], U16, name="offsets")
         nc.sync.dma_start(offsets[:], offs)
         raw_words = keep([P, 3, 2 * N], U8, "raw_words")
-        weight = keep([P, J], F32, "weight")
-        x_rows = xT.rearrange("(a p i) t -> a i p t", a=2, i=4)
-        planes = [keep([P, T], F32, "plane%d" % u) for u in range(8)]
-        c_parts = [slice(0, Q), slice(Q, H), SECOND]
-        c_raw = [keep([P, 4, width(part)], F32, "c_raw%d" % q) for q, part in enumerate(c_parts)]
-        wd_raw = [keep([P, 4, N], F32, "wd_raw%d" % a) for a in range(2)]
-        c_rows = c.rearrange("(p i) j -> p i j", i=4)
-        wd_rows = wtd.rearrange("(a p i) n -> a p i n", a=2, i=4)
+        weight = [keep([P, H], F32, "weight%d" % h) for h in range(2)]
+        planes = [keep([P, T], F32, "plane%d" % u) for u in range(2 * PACK)]
+        c_raw = [keep([P, PACK, width(part)], F32, "c_raw%d" % n) for n, part in enumerate(C_PARTS)]
+        wd_raw = [keep([P, PACK, N], F32, "wd_raw%d" % a) for a in range(2)]
+        bias = keep([P, PACK], F32, "bias")
+        x_rows = xT.rearrange("(a p i) t -> a i p t", a=2, i=PACK)
+        c_rows = c.rearrange("(p i) j -> p i j", i=PACK)
+        wd_rows = wtd.rearrange("(a p i) n -> a p i n", a=2, i=PACK)
 
-        def load_x(u):
-            nc.sync.dma_start(out=planes[u][:], in_=x_rows[u // 4, u % 4])
+        def load_plane(u):
+            nc.sync.dma_start(out=planes[u][:], in_=x_rows[u // PACK, u % PACK])
 
-        def load_c(q):
-            nc.sync.dma_start(out=c_raw[q][:], in_=c_rows[:, :, c_parts[q]])
+        def load_c(n):
+            nc.sync.dma_start(out=c_raw[n][:], in_=c_rows[:, :, C_PARTS[n]])
 
         def load_wd(a):
             nc.sync.dma_start(out=wd_raw[a][:], in_=wd_rows[a])
 
-        def load_scales(q):
+        def load_scales(quad):
+            live, rows = slice(32 * quad, 32 * quad + 4), slice(4 * quad, 4 * quad + 4)
+            nc.sync.dma_start(out=raw_scales[live, 2, :].bitcast(I32), in_=wx_scales[0, rows, :].bitcast(I32))
             nc.sync.dma_start(
-                out=raw_scales[32 * q : 32 * q + 4, 2, :].bitcast(I32),
-                in_=wx_scales[0, 4 * q : 4 * q + 4, :].bitcast(I32),
-            )
-            nc.sync.dma_start(
-                out=raw_scales[32 * q : 32 * q + 4, 0:2, :].bitcast(I32),
-                in_=wt4_scales[:, 4 * q : 4 * q + 4, :].rearrange("a r n -> r a n").bitcast(I32),
+                out=raw_scales[live, 0:2, :].bitcast(I32),
+                in_=wt4_scales[:, rows, :].rearrange("a r n -> r a n").bitcast(I32),
             )
 
         load_c(0)
         load_c(1)
         nc.sync.dma_start(out=raw_words[:, 0:2, :].bitcast(I32), in_=wt4_words.rearrange("a p n -> p a n").bitcast(I32))
         nc.sync.dma_start(out=raw_words[:, 2, :].bitcast(I32), in_=wx_words[0].bitcast(I32))
-        nc.sync.dma_start(out=weight[:], in_=wgt)
-        load_x(0)
-        load_scales(0)
-        load_x(1)
-        load_scales(1)
-        load_x(2)
-        load_scales(2)
-        load_x(3)
-        load_scales(3)
+        for h in range(2):
+            nc.sync.dma_start(out=weight[h][:], in_=wgt[:, HALVES[h]])
+        for u in range(PACK):
+            load_plane(u)
+            load_scales(u)
         load_c(2)
         load_wd(0)
-        nc.sync.dma_start(out=bias[:], in_=b.rearrange("(p t) -> p t", t=4))
-        load_x(4)
+        nc.sync.dma_start(out=bias[:], in_=b.rearrange("(p t) -> p t", t=PACK))
+        load_plane(PACK)
         load_wd(1)
-        for u in range(5, 8):
-            load_x(u)
+        for u in range(PACK + 1, 2 * PACK):
+            load_plane(u)
 
-        def operand(name):
-            return keep([P, J], U32, name + "_codes"), keep([P, J], U8, name + "_scales")
-
-        def quantise(dst, part, src):
-            nc.vector.quantize_mx(out=dst[0][:, part].bitcast(E4M3), scales=dst[1][:, part], in_=src)
-
-        def staged(columns):
-            return stage.tile([P, 4 * H], BF16, name="staged", tag="staged", align_bytes=64)[:, 0 : 4 * columns]
-
-        def copy_on(engine, out, in_):
-            if engine == "vector":
-                nc.vector.tensor_copy(out=out, in_=in_)
-            else:
-                nc.scalar.copy(out=out, in_=in_)
-
-        def woven(dst):
-            return dst.rearrange("p (c e i) -> p c i e", e=RUN, i=4)
-
-        def by_plane(src):
-            return src.rearrange("p i (c e) -> p c i e", e=RUN)
-
-        def four(flat):
-            return flat.rearrange("p (i j) -> p i j", i=4)
-
-        eye = keep([P, H], U32, "eye_codes"), keep([P, H], U8, "eye_scales")
-        quantise(eye, FIRST, ident[:])
-
-        cq = {0: (keep([P, H], U32, "cq0"), keep([P, H], U8, "cqs0"))}
-        cr = [(keep([P, H], U32, "cr%d" % h), keep([P, H], U8, "crs%d" % h)) for h in range(2)]
-        wd = {0: (keep([P, H], U32, "wd0"), keep([P, H], U8, "wds0")), 1: (keep([P, H], U32, "wd1"), keep([P, H], U8, "wds1"))}
-        xq = {(a, h): (keep([P, H], U32, "xq%d%d" % (a, h)), keep([P, H], U8, "xqs%d%d" % (a, h)))
-              for a in range(2) for h in range(2)}
+        cq = {0: operand("cq0")}
+        cr = [operand("cr%d" % h) for h in range(2)]
+        wd = [operand("wd%d" % a) for a in range(2)]
+        xq = {(a, h): operand("xq%d%d" % (a, h)) for a in range(2) for h in range(2)}
 
         def gather(u, part, dst):
-            n = width(part)
-            i = u % 4
             nc.vector.tensor_tensor(
-                dst[:, i * n : (i + 1) * n],
+                dst,
                 planes[u][:].indirect(offsets[:, part.start // 16 : part.stop // 16]),
-                weight[:, part],
+                weight[part.start // H][:, in_half(part)],
                 ALU.mult,
             )
 
-        def bank(n):
-            return psum.tile([P, H], F32, name="bank", tag="bank%d" % n)
+        def gather_late(u, name, picked):
+            n = width(CHUNKS[name])
+            gather(u, CHUNKS[name], picked[:, (u - PACK) * n : (u - PACK + 1) * n])
 
-        def first_tier(q, engine, rounded):
-            copy_on(engine, woven(rounded), by_plane(c_raw[q][:]))
-            quantise(cq[q // 2], local(c_parts[q]), rounded)
+        def first_tier(n, engine, rounded):
+            round_on(engine, woven(rounded), by_row(c_raw[n][:]))
+            quantise(cq[C_PARTS[n].start // H], in_half(C_PARTS[n]), rounded)
 
-        def second_tier(h, rest):
-            for s in range(4):
-                part = slice(s * P, (s + 1) * P)
-                back = bank(4 + s)
-                for i in range(4):
+        def second_tier(h, sources, first_bank, rest):
+            for s in range(H // P):
+                back = bank(first_bank + s)
+                for i in range(PACK):
                     nc.tensor.matmul_mx(
-                        out=back[:, i * P : (i + 1) * P],
-                        lhsT=eye[0][:, i * P : (i + 1) * P].bitcast(E4M3),
-                        lhsT_scale=eye[1][:, i * P : (i + 1) * P],
-                        rhs=cq[h][0][:, part].bitcast(E4M3),
-                        rhs_scale=cq[h][1][:, part],
+                        out=back[:, block(i)], lhsT=eye[0][:, block(i)].bitcast(E4M3), lhsT_scale=eye[1][:, block(i)],
+                        rhs=cq[h][0][:, block(s)].bitcast(E4M3), rhs_scale=cq[h][1][:, block(s)],
                         start=True, stop=True,
                     )
                 nc.vector.tensor_tensor(
-                    woven(rest[:, s * 4 * P : (s + 1) * 4 * P]),
-                    by_plane(c_raw[2][:, :, part] if h else c_raw[s // 2][:, :, s % 2 * P : (s % 2 + 1) * P]),
-                    by_plane(four(back[:])),
+                    woven(rest[:, s * PACK * P : (s + 1) * PACK * P]), by_row(sources[s]), by_row(four_rows(back[:])),
                     ALU.subtract,
                 )
-            quantise(cr[h], FIRST, rest)
+            quantise(cr[h], slice(0, H), rest)
 
         def change(a, rounded):
-            copy_on(
-                "scalar",
-                rounded.rearrange("p (s t m i) -> p s m i t", s=2, t=2, i=4),
-                wd_raw[a][:].rearrange("p i (m s t) -> p s m i t", s=2, t=2),
+            nc.scalar.copy(
+                out=rounded.rearrange("p (s t m i) -> p s m i t", s=2, t=2, i=PACK),
+                in_=wd_raw[a][:].rearrange("p i (m s t) -> p s m i t", s=2, t=2),
             )
-            quantise(wd[a], FIRST, rounded)
+            quantise(wd[a], slice(0, N), rounded)
 
-        def local(part):
-            return slice(part.start % H, (part.stop - 1) % H + 1)
-
-        def picks(a, part, src, engine, rounded):
-            copy_on(engine, woven(rounded), by_plane(src))
-            quantise(xq[a, part.start // H], local(part), rounded)
+        def picks(a, part, picked, engine, rounded):
+            round_on(engine, woven(rounded), by_row(picked))
+            quantise(xq[a, part.start // H], in_half(part), rounded)
 
         acc = {}
 
         def open_chunk(name):
             tiles = {n: bank(n) for n in sorted(set(BANKS[name]))}
             n = width(CHUNKS[name])
-            for t in range(4):
-                at = (t * n) % H
+            for t in range(PACK):
+                at = t * n % H
                 acc[name, t] = tiles[BANKS[name][t]][:, at : at + n]
 
-        def mx_pass(name, t, fixed, fixed_scale, moving, step, start=False, stop=False):
-            part = local(CHUNKS[name])
-            starts = list(range(0, width(part), step))
-            for at in starts:
+        def mx_passes(name, t, fixed, fixed_scale, moving, step, start=False, stop=False):
+            part = in_half(CHUNKS[name])
+            for at in range(0, width(part), step):
                 cols = slice(part.start + at, part.start + at + step)
                 nc.tensor.matmul_mx(
                     out=acc[name, t][:, at : at + step], lhsT=fixed, lhsT_scale=fixed_scale,
                     rhs=moving[0][:, cols].bitcast(E4M3), rhs_scale=moving[1][:, cols],
-                    start=start and at == starts[0], stop=stop and at == starts[-1],
+                    start=start and at == 0, stop=stop and at + step == width(part),
                 )
 
-        def fp4_pass(name, t, words, plane, moving, start=False):
-            mx_pass(name, t, words[:, 2 * P * t : 2 * P * (t + 1)].bitcast(E2M1),
-                    fp4_scales[:, plane, t * P : (t + 1) * P], moving, H if name == "A" else P, start=start)
+        def fp4_passes(name, t, which, moving, start=False):
+            words = fp4_words[:, which, 2 * P * t : 2 * P * (t + 1)].bitcast(E2M1)
+            mx_passes(name, t, words, fp4_scales[:, which, block(t)], moving, FP4_STEP[name], start=start)
 
-        def own_passes(name):
-            open_chunk(name)
-            h = CHUNKS[name].start // H
-            for t in range(4):
-                opens = t == 0 or BANKS[name][t] != BANKS[name][t - 1]
-                fp4_pass(name, t, fp4_words[:, 2, :], 2, cq[h], start=opens)
-                fp4_pass(name, t, fp4_words[:, 2, :], 2, cr[h])
+        def tier_passes(name, tier, opening):
+            for t in range(PACK):
+                first_in_bank = t == 0 or BANKS[name][t] != BANKS[name][t - 1]
+                fp4_passes(name, t, 2, tier[CHUNKS[name].start // H], start=opening and first_in_bank)
 
         def pick_passes(a, name):
             moving = xq[a, CHUNKS[name].start // H]
-            for t in range(4):
-                closes = a == 1 and (t == 3 or BANKS[name][t] != BANKS[name][t + 1])
-                fp4_pass(name, t, fp4_words[:, a, :], a, moving)
-                mx_pass(name, t, wd[a][0][:, t * P : (t + 1) * P].bitcast(E4M3), wd[a][1][:, t * P : (t + 1) * P],
-                        moving, width(CHUNKS[name]), stop=closes)
+            for t in range(PACK):
+                last_in_bank = t == PACK - 1 or BANKS[name][t] != BANKS[name][t + 1]
+                fp4_passes(name, t, a, moving)
+                mx_passes(name, t, wd[a][0][:, block(t)].bitcast(E4M3), wd[a][1][:, block(t)], moving,
+                          width(CHUNKS[name]), stop=a == 1 and last_in_bank)
 
-        y_rows = out_0.rearrange("(p t) j -> p t j", t=4)
+        y_rows = out_0.rearrange("(p t) j -> p t j", t=PACK)
         y_words = out_1[0].rearrange("p j i -> p (j i)").bitcast(I32)
-        y_mx = operand("y")
-        y = {name: keep([P, 4, width(part)], F32, "y" + name) for name, part in CHUNKS.items()}
+        y_mx = operand("y", J)
+        y = {name: keep([P, PACK, width(part)], F32, "y" + name) for name, part in CHUNKS.items()}
 
         def finish(name):
-            part = CHUNKS[name]
-            for t in range(4):
+            per_bank = H // width(CHUNKS[name])
+            for t in range(PACK):
                 nc.scalar.activation(y[name][:, t, :], acc[name, t], ACT.Silu, bias=bias[:, t : t + 1])
-                if name == "A":
-                    nc.sync.dma_start(out=y_rows[:, t, part], in_=y[name][:, t, :])
-                elif t % 2 == 1:
-                    nc.sync.dma_start(out=y_rows[:, t - 1 : t + 1, part], in_=y[name][:, t - 1 : t + 1, :])
+                if (t + 1) % per_bank == 0:
+                    rows = slice(t + 1 - per_bank, t + 1)
+                    nc.sync.dma_start(out=y_rows[:, rows, CHUNKS[name]], in_=y[name][:, rows, :])
 
         def hand_on(name, engine):
             part = CHUNKS[name]
             rounded = staged(width(part))
-            copy_on(engine, woven(rounded), by_plane(y[name][:]))
+            round_on(engine, woven(rounded), by_row(y[name][:]))
             quantise(y_mx, part, rounded)
             nc.sync.dma_start(out=y_words[:, part], in_=y_mx[0][:, part].bitcast(I32))
 
-        whole = slice(0, J)
-        rounded_c = keep([P, 4 * H], BF16, "rounded_c", tag="ident")
-        first_tier(0, "vector", rounded_c[:, 0 : 4 * Q])
-        first_tier(1, "vector", rounded_c[:, 4 * Q : 4 * H])
+        rounded_c = staged_in("ident", "rounded_c")
+        first_tier(0, "vector", rounded_c[:, 0 : PACK * Q])
+        first_tier(1, "vector", rounded_c[:, PACK * Q : PACK * H])
         fp4_words = keep([P, 3, 2 * N], U8, "fp4_words", tag="ident")
         nc.vector.tensor_copy(
-            out=fp4_words[:].bitcast(U16).rearrange("p a (t m) -> p t a m", t=4),
-            in_=raw_words[:].bitcast(U16).rearrange("p a (m t) -> p t a m", t=4),
+            out=fp4_words[:].bitcast(U16).rearrange("p a (t m) -> p t a m", t=PACK),
+            in_=raw_words[:].bitcast(U16).rearrange("p a (m t) -> p t a m", t=PACK),
         )
-        second_tier(0, keep([P, 4 * H], BF16, "rest0", tag="low")[:])
-        low = keep([P, 4 * J], F32, "low")
-        for u in range(4):
-            gather(u, whole, low)
-        spent = keep([P, 4 * H + 3 * N], U8, "spent", tag="plane3")
-        cq[1] = spent[:, 0 : 4 * H].bitcast(U32), keep([P, H], U8, "cqs1")
-        first_tier(2, "scalar", keep([P, 4 * H], BF16, "rounded_c2", tag="high_a")[:])
-        fp4_scales = spent[:, 4 * H : 4 * H + 3 * N].rearrange("p (a n) -> p a n", a=3)
+        quarters = [c_raw[s // 2][:, :, block(s % 2)] for s in range(H // P)]
+        second_tier(0, quarters, BANKS["B"][0], staged_in("early", "rest0"))
+
+        early = keep([P, PACK * J], F32, "early")
+        for u in range(PACK):
+            for half in HALVES:
+                gather(u, half, four_rows(early[:])[:, u, half])
+
+        spent = keep([P, PACK * H + 3 * N], U8, "spent", tag="plane3")
+        cq[1] = spent[:, 0 : PACK * H].bitcast(U32), keep([P, H], U8, "cq1_scales")
+        first_tier(2, "scalar", staged_in("turn", "rounded_c2"))
+        fp4_scales = spent[:, PACK * H :].rearrange("p (a n) -> p a n", a=3)
         nc.vector.tensor_copy(
-            out=fp4_scales.rearrange("p a (t m) -> p t a m", t=4),
-            in_=raw_scales[:].rearrange("p a (m t) -> p t a m", t=4),
+            out=fp4_scales.rearrange("p a (t m) -> p t a m", t=PACK),
+            in_=raw_scales[:].rearrange("p a (m t) -> p t a m", t=PACK),
         )
-        high_a = keep([P, 7 * H], F32, "high_a")
-        gather(4, FIRST, high_a)
-        second_tier(1, high_a[:, H : 3 * H].bitcast(BF16))
-        own_passes("A")
-        own_passes("B")
-        own_passes("C")
-        change(0, high_a[:, 5 * H : 7 * H].bitcast(BF16))
-        change(1, keep([P, 4 * H], BF16, "rounded_wd1", tag="wd_raw0")[:])
-        gather(5, FIRST, high_a)
-        picks(0, FIRST, four(low[:])[:, :, FIRST], "scalar", keep([P, 4 * H], BF16, "rounded_low", tag="wd_raw1")[:])
+        late_a = keep([P, PACK * H], F32, "late_a", tag="raw_scales")
+        gather_late(4, "A", late_a)
+        second_tier(1, [c_raw[2][:, :, block(s)] for s in range(H // P)], BANKS["A"][0],
+                    late_a[:, 3 * Q : 7 * Q].bitcast(BF16))
+        for name in "BCA":
+            open_chunk(name)
+            tier_passes(name, cq, True)
+        for name in "ABC":
+            tier_passes(name, cr, False)
+
+        change(0, staged_in("turn", "rounded_wd0"))
+        picks(0, HALVES[0], four_rows(early[:])[:, :, HALVES[0]], "scalar", staged_in("wd_raw0", "rounded_x0"))
         pick_passes(0, "A")
-        gather(6, FIRST, high_a)
-        picks(0, SECOND, four(low[:])[:, :, SECOND], "scalar", high_a[:, 3 * H : 5 * H].bitcast(BF16))
+        gather_late(5, "A", late_a)
+        change(1, staged_in("c_raw2", "rounded_wd1"))
+        gather_late(6, "A", late_a)
+        picks(0, HALVES[1], four_rows(early[:])[:, :, HALVES[1]], "scalar", staged_in("wd_raw1", "rounded_x1"))
         pick_passes(0, "B")
         pick_passes(0, "C")
-        gather(7, FIRST, high_a)
-        high_b = keep([P, 4 * Q], F32, "high_b", tag="low")
-        for u in range(4, 8):
-            gather(u, CHUNKS["B"], high_b)
-        picks(1, FIRST, four(high_a[:, 0 : 4 * H]), "scalar", keep([P, 4 * H], BF16, "rounded_a", tag="late")[:])
+        gather_late(7, "A", late_a)
+
+        late_b = keep([P, PACK * Q], F32, "late_b", tag="weight0")
+        for u in range(PACK, 2 * PACK):
+            gather_late(u, "B", late_b)
+        picks(1, CHUNKS["A"], four_rows(late_a[:]), "scalar", staged_in("late_c", "rounded_a"))
         pick_passes(1, "A")
-        high_c = keep([P, 4 * Q], F32, "high_c", tag="late")
-        gather(4, CHUNKS["C"], high_c)
-        gather(5, CHUNKS["C"], high_c)
-        picks(1, CHUNKS["B"], four(high_b[:]), "scalar", high_c[:, 2 * Q : 4 * Q].bitcast(BF16))
-        gather(6, CHUNKS["C"], high_c)
-        gather(7, CHUNKS["C"], high_c)
+        picks(1, CHUNKS["B"], four_rows(late_b[:]), "scalar", staged(Q))
+        late_c = keep([P, PACK * Q], F32, "late_c")
+        for u in range(PACK, 2 * PACK):
+            gather_late(u, "C", late_c)
         finish("A")
         pick_passes(1, "B")
-        picks(1, CHUNKS["C"], four(high_c[:]), "vector", staged(Q))
+        picks(1, CHUNKS["C"], four_rows(late_c[:]), "vector", staged(Q))
         pick_passes(1, "C")
         hand_on("A", "vector")
         finish("B")
         finish("C")
         hand_on("C", "vector")
         hand_on("B", "scalar")
-        for q in range(4):
-            queue = nc.sync if q % 2 == 0 else nc.scalar
+        for quad in range(4):
+            queue = nc.sync if quad % 2 == 0 else nc.scalar
             queue.dma_start(
-                out=out_2[0, 4 * q : 4 * q + 4, :].bitcast(I32),
-                in_=y_mx[1][32 * q : 32 * q + 4, :].bitcast(I32),
+                out=out_2[0, 4 * quad : 4 * quad + 4, :].bitcast(I32),
+                in_=y_mx[1][32 * quad : 32 * quad + 4, :].bitcast(I32),
             )

from contextlib import ExitStack

import concourse.mybir as mybir

K, L, N, T, J = 1024, 512, 512, 2048, 1024
FLOPS = 2 * N * J * (2 * K + 2 * L) + 2 * L * L * J

F32 = mybir.dt.float32
BF16 = mybir.dt.bfloat16
I32 = mybir.dt.int32
U32 = mybir.dt.uint32
U16 = mybir.dt.uint16
U8 = mybir.dt.uint8
E4M3 = mybir.dt.float8_e4m3fn_x4
E2M1 = mybir.dt.float4_e2m1fn_x4
ALU = mybir.AluOpType
ACT = mybir.ActivationFunctionType

P = 128
PACK = 4
H = J // 2
Q = J // 4
HALVES = (slice(0, H), slice(H, J))
CHUNKS = {"A": slice(0, H), "B": slice(H, H + Q), "C": slice(H + Q, J)}
BANKS = {"A": (0, 1, 2, 3), "B": (4, 4, 5, 5), "C": (6, 6, 7, 7)}
FP4_STEP = {"A": H, "B": P, "C": P}
C_PARTS = (slice(0, Q), slice(Q, H), slice(H, J))
STAGING_BUFS = 5


def width(part):
    return part.stop - part.start


def in_half(part):
    return slice(part.start % H, (part.stop - 1) % H + 1)


def block(n):
    return slice(n * P, (n + 1) * P)


def woven(dst):
    return dst.rearrange("p (c e i) -> p c i e", e=2, i=PACK)


def by_row(src):
    return src.rearrange("p i (c e) -> p c i e", e=2)


def four_rows(flat):
    return flat.rearrange("p (i j) -> p i j", i=PACK)


def tile_list_dl_siluP_kernel(
    tc, xT, wgt, wt4_words, wt4_scales, wtd, c, wx_words, wx_scales, b, offs, out_0, out_1, out_2
):
    nc = tc.nc
    with ExitStack() as ctx:
        held = ctx.enter_context(tc.tile_pool(name="held", bufs=1))
        stage = ctx.enter_context(tc.tile_pool(name="stage", bufs=STAGING_BUFS))
        psum = ctx.enter_context(tc.psum_pool(name="psum", bufs=1))

        def keep(shape, dtype, name, tag=None):
            return held.tile(shape, dtype, name=name, tag=tag or name, align_bytes=64)

        def staged(columns):
            return stage.tile([P, PACK * H], BF16, name="staged", tag="staged", align_bytes=64)[:, 0 : PACK * columns]

        def staged_in(tag, name):
            return keep([P, PACK * H], BF16, name, tag=tag)[:]

        def operand(name, columns=H):
            return keep([P, columns], U32, name + "_codes"), keep([P, columns], U8, name + "_scales")

        def bank(n):
            return psum.tile([P, H], F32, name="bank", tag="bank%d" % n)

        def quantise(dst, part, src):
            nc.vector.quantize_mx(out=dst[0][:, part].bitcast(E4M3), scales=dst[1][:, part], in_=src)

        def round_on(engine, out, in_):
            if engine == "vector":
                nc.vector.tensor_copy(out=out, in_=in_)
            else:
                nc.scalar.copy(out=out, in_=in_)

        raw_scales = keep([P, 3, N], U8, "raw_scales")
        nc.vector.memset(raw_scales[:].rearrange("p a n -> p (a n)").bitcast(I32), 0)

        seed = keep([P, L + PACK], BF16, "seed")
        nc.gpsimd.memset(seed[:], 0.0)
        nc.gpsimd.affine_select(
            out=seed[:], in_=seed[:], pattern=[[1, L + PACK]],
            compare_op=ALU.not_equal, fill=1.0, base=1 - PACK, channel_multiplier=-PACK,
        )
        ident = keep([P, PACK * L], BF16, "ident")
        for i in range(PACK):
            nc.vector.tensor_copy(out=ident[:, i * L : (i + 1) * L], in_=seed[:, PACK - 1 - i : PACK - 1 - i + L])
        eye = operand("eye")
        quantise(eye, slice(0, L), ident[:])

        offsets = held.tile([P, J // 16], U16, name="offsets")
        nc.sync.dma_start(offsets[:], offs)
        raw_words = keep([P, 3, 2 * N], U8, "raw_words")
        weight = [keep([P, H], F32, "weight%d" % h) for h in range(2)]
        planes = [keep([P, T], F32, "plane%d" % u) for u in range(2 * PACK)]
        c_raw = [keep([P, PACK, width(part)], F32, "c_raw%d" % n) for n, part in enumerate(C_PARTS)]
        wd_raw = [keep([P, PACK, N], F32, "wd_raw%d" % a) for a in range(2)]
        bias = keep([P, PACK], F32, "bias")
        x_rows = xT.rearrange("(a p i) t -> a i p t", a=2, i=PACK)
        c_rows = c.rearrange("(p i) j -> p i j", i=PACK)
        wd_rows = wtd.rearrange("(a p i) n -> a p i n", a=2, i=PACK)

        def load_plane(u):
            nc.sync.dma_start(out=planes[u][:], in_=x_rows[u // PACK, u % PACK])

        def load_c(n):
            nc.sync.dma_start(out=c_raw[n][:], in_=c_rows[:, :, C_PARTS[n]])

        def load_wd(a):
            nc.sync.dma_start(out=wd_raw[a][:], in_=wd_rows[a])

        def load_scales(quad):
            live, rows = slice(32 * quad, 32 * quad + 4), slice(4 * quad, 4 * quad + 4)
            nc.sync.dma_start(out=raw_scales[live, 2, :].bitcast(I32), in_=wx_scales[0, rows, :].bitcast(I32))
            nc.sync.dma_start(
                out=raw_scales[live, 0:2, :].bitcast(I32),
                in_=wt4_scales[:, rows, :].rearrange("a r n -> r a n").bitcast(I32),
            )

        load_c(0)
        load_c(1)
        nc.sync.dma_start(out=raw_words[:, 0:2, :].bitcast(I32), in_=wt4_words.rearrange("a p n -> p a n").bitcast(I32))
        nc.sync.dma_start(out=raw_words[:, 2, :].bitcast(I32), in_=wx_words[0].bitcast(I32))
        for h in range(2):
            nc.sync.dma_start(out=weight[h][:], in_=wgt[:, HALVES[h]])
        for u in range(PACK):
            load_plane(u)
            load_scales(u)
        load_c(2)
        load_wd(0)
        nc.sync.dma_start(out=bias[:], in_=b.rearrange("(p t) -> p t", t=PACK))
        load_plane(PACK)
        load_wd(1)
        for u in range(PACK + 1, 2 * PACK):
            load_plane(u)

        cq = {0: operand("cq0")}
        cr = [operand("cr%d" % h) for h in range(2)]
        wd = [operand("wd%d" % a) for a in range(2)]
        xq = {(a, h): operand("xq%d%d" % (a, h)) for a in range(2) for h in range(2)}

        def gather(u, part, dst):
            nc.vector.tensor_tensor(
                dst,
                planes[u][:].indirect(offsets[:, part.start // 16 : part.stop // 16]),
                weight[part.start // H][:, in_half(part)],
                ALU.mult,
            )

        def gather_late(u, name, picked):
            n = width(CHUNKS[name])
            gather(u, CHUNKS[name], picked[:, (u - PACK) * n : (u - PACK + 1) * n])

        def first_tier(n, engine, rounded):
            round_on(engine, woven(rounded), by_row(c_raw[n][:]))
            quantise(cq[C_PARTS[n].start // H], in_half(C_PARTS[n]), rounded)

        def second_tier(h, sources, first_bank, rest):
            for s in range(H // P):
                back = bank(first_bank + s)
                for i in range(PACK):
                    nc.tensor.matmul_mx(
                        out=back[:, block(i)], lhsT=eye[0][:, block(i)].bitcast(E4M3), lhsT_scale=eye[1][:, block(i)],
                        rhs=cq[h][0][:, block(s)].bitcast(E4M3), rhs_scale=cq[h][1][:, block(s)],
                        start=True, stop=True,
                    )
                nc.vector.tensor_tensor(
                    woven(rest[:, s * PACK * P : (s + 1) * PACK * P]), by_row(sources[s]), by_row(four_rows(back[:])),
                    ALU.subtract,
                )
            quantise(cr[h], slice(0, H), rest)

        def change(a, rounded):
            nc.scalar.copy(
                out=rounded.rearrange("p (s t m i) -> p s m i t", s=2, t=2, i=PACK),
                in_=wd_raw[a][:].rearrange("p i (m s t) -> p s m i t", s=2, t=2),
            )
            quantise(wd[a], slice(0, N), rounded)

        def picks(a, part, picked, engine, rounded):
            round_on(engine, woven(rounded), by_row(picked))
            quantise(xq[a, part.start // H], in_half(part), rounded)

        acc = {}

        def open_chunk(name):
            tiles = {n: bank(n) for n in sorted(set(BANKS[name]))}
            n = width(CHUNKS[name])
            for t in range(PACK):
                at = t * n % H
                acc[name, t] = tiles[BANKS[name][t]][:, at : at + n]

        def mx_passes(name, t, fixed, fixed_scale, moving, step, start=False, stop=False):
            part = in_half(CHUNKS[name])
            for at in range(0, width(part), step):
                cols = slice(part.start + at, part.start + at + step)
                nc.tensor.matmul_mx(
                    out=acc[name, t][:, at : at + step], lhsT=fixed, lhsT_scale=fixed_scale,
                    rhs=moving[0][:, cols].bitcast(E4M3), rhs_scale=moving[1][:, cols],
                    start=start and at == 0, stop=stop and at + step == width(part),
                )

        def fp4_passes(name, t, which, moving, start=False):
            words = fp4_words[:, which, 2 * P * t : 2 * P * (t + 1)].bitcast(E2M1)
            mx_passes(name, t, words, fp4_scales[:, which, block(t)], moving, FP4_STEP[name], start=start)

        def tier_passes(name, tier, opening):
            for t in range(PACK):
                first_in_bank = t == 0 or BANKS[name][t] != BANKS[name][t - 1]
                fp4_passes(name, t, 2, tier[CHUNKS[name].start // H], start=opening and first_in_bank)

        def pick_passes(a, name):
            moving = xq[a, CHUNKS[name].start // H]
            for t in range(PACK):
                last_in_bank = t == PACK - 1 or BANKS[name][t] != BANKS[name][t + 1]
                fp4_passes(name, t, a, moving)
                mx_passes(name, t, wd[a][0][:, block(t)].bitcast(E4M3), wd[a][1][:, block(t)], moving,
                          width(CHUNKS[name]), stop=a == 1 and last_in_bank)

        y_rows = out_0.rearrange("(p t) j -> p t j", t=PACK)
        y_words = out_1[0].rearrange("p j i -> p (j i)").bitcast(I32)
        y_mx = operand("y", J)
        y = {name: keep([P, PACK, width(part)], F32, "y" + name) for name, part in CHUNKS.items()}

        def finish(name):
            per_bank = H // width(CHUNKS[name])
            for t in range(PACK):
                nc.scalar.activation(y[name][:, t, :], acc[name, t], ACT.Silu, bias=bias[:, t : t + 1])
                if (t + 1) % per_bank == 0:
                    rows = slice(t + 1 - per_bank, t + 1)
                    nc.sync.dma_start(out=y_rows[:, rows, CHUNKS[name]], in_=y[name][:, rows, :])

        def hand_on(name, engine):
            part = CHUNKS[name]
            rounded = staged(width(part))
            round_on(engine, woven(rounded), by_row(y[name][:]))
            quantise(y_mx, part, rounded)
            nc.sync.dma_start(out=y_words[:, part], in_=y_mx[0][:, part].bitcast(I32))

        rounded_c = staged_in("ident", "rounded_c")
        first_tier(0, "vector", rounded_c[:, 0 : PACK * Q])
        first_tier(1, "vector", rounded_c[:, PACK * Q : PACK * H])
        fp4_words = keep([P, 3, 2 * N], U8, "fp4_words", tag="ident")
        nc.vector.tensor_copy(
            out=fp4_words[:].bitcast(U16).rearrange("p a (t m) -> p t a m", t=PACK),
            in_=raw_words[:].bitcast(U16).rearrange("p a (m t) -> p t a m", t=PACK),
        )
        quarters = [c_raw[s // 2][:, :, block(s % 2)] for s in range(H // P)]
        second_tier(0, quarters, BANKS["B"][0], staged_in("early", "rest0"))

        early = keep([P, PACK * J], F32, "early")
        for u in range(PACK):
            for half in HALVES:
                gather(u, half, four_rows(early[:])[:, u, half])

        spent = keep([P, PACK * H + 3 * N], U8, "spent", tag="plane3")
        cq[1] = spent[:, 0 : PACK * H].bitcast(U32), keep([P, H], U8, "cq1_scales")
        first_tier(2, "scalar", staged_in("turn", "rounded_c2"))
        fp4_scales = spent[:, PACK * H :].rearrange("p (a n) -> p a n", a=3)
        nc.vector.tensor_copy(
            out=fp4_scales.rearrange("p a (t m) -> p t a m", t=PACK),
            in_=raw_scales[:].rearrange("p a (m t) -> p t a m", t=PACK),
        )
        late_a = keep([P, PACK * H], F32, "late_a", tag="raw_scales")
        gather_late(4, "A", late_a)
        second_tier(1, [c_raw[2][:, :, block(s)] for s in range(H // P)], BANKS["A"][0],
                    late_a[:, 3 * Q : 7 * Q].bitcast(BF16))
        for name in "BCA":
            open_chunk(name)
            tier_passes(name, cq, True)
        for name in "ABC":
            tier_passes(name, cr, False)

        change(0, staged_in("turn", "rounded_wd0"))
        picks(0, HALVES[0], four_rows(early[:])[:, :, HALVES[0]], "scalar", staged_in("wd_raw0", "rounded_x0"))
        pick_passes(0, "A")
        gather_late(5, "A", late_a)
        change(1, staged_in("c_raw2", "rounded_wd1"))
        gather_late(6, "A", late_a)
        picks(0, HALVES[1], four_rows(early[:])[:, :, HALVES[1]], "scalar", staged_in("wd_raw1", "rounded_x1"))
        pick_passes(0, "B")
        pick_passes(0, "C")
        gather_late(7, "A", late_a)

        late_b = keep([P, PACK * Q], F32, "late_b", tag="weight0")
        for u in range(PACK, 2 * PACK):
            gather_late(u, "B", late_b)
        picks(1, CHUNKS["A"], four_rows(late_a[:]), "scalar", staged_in("late_c", "rounded_a"))
        pick_passes(1, "A")
        picks(1, CHUNKS["B"], four_rows(late_b[:]), "scalar", staged(Q))
        late_c = keep([P, PACK * Q], F32, "late_c")
        for u in range(PACK, 2 * PACK):
            gather_late(u, "C", late_c)
        finish("A")
        pick_passes(1, "B")
        picks(1, CHUNKS["C"], four_rows(late_c[:]), "vector", staged(Q))
        pick_passes(1, "C")
        hand_on("A", "vector")
        finish("B")
        finish("C")
        hand_on("C", "vector")
        hand_on("B", "scalar")
        for quad in range(4):
            queue = nc.sync if quad % 2 == 0 else nc.scalar
            queue.dma_start(
                out=out_2[0, 4 * quad : 4 * quad + 4, :].bitcast(I32),
                in_=y_mx[1][32 * quad : 32 * quad + 4, :].bitcast(I32),
            )
